import numpy as np
import ml_dtypes


def mxq(x, axis, fmt="e4m3"):
    dtype, down = {"e4m3": (ml_dtypes.float8_e4m3fn, 7), "e5m2": (ml_dtypes.float8_e5m2, 14)}[fmt]
    v = np.moveaxis(np.asarray(x, np.float32).astype(ml_dtypes.bfloat16).astype(np.float64), axis, -1)
    blocks = v.reshape(v.shape[:-1] + (-1, 32))
    amax = np.abs(blocks).max(-1, keepdims=True)
    byte = np.maximum(np.where(amax > 0, np.frexp(amax)[1] - 1 + 127, 0) - down, 1)
    scale = np.exp2(byte - 127.0)
    codes = (blocks / scale).astype(np.float32).astype(dtype).astype(np.float64)
    return np.moveaxis((codes * scale).reshape(v.shape), -1, axis)


WIDE = False


def mx_kscale(k):
    if not WIDE:
        return np.ones(k)
    levels = np.array([10, -10, 5, -5, 0])
    if k % 512:
        return np.exp2(np.random.permutation(np.resize(levels, k // 32))).repeat(32)
    a = np.empty((k // 512, 16))
    for p in range(k // 512):
        a[p, :8] = np.random.permutation(np.resize(levels, 8))
        for g in range(8):
            far = levels[np.abs(levels - a[p, g]) >= 10]
            a[p, g + 8] = far[np.random.randint(len(far))]
    return np.exp2(a.ravel()).repeat(32)


def f64(x):
    return np.asarray(x).astype(np.float64)


def striped(idx):
    return np.tile(np.asarray(idx).reshape(-1, 16).T, (8, 1)).astype(np.uint16)


def unstriped(offs):
    return offs[:16].T.reshape(-1).astype(np.int64)


E2M1 = np.array([0.0, 0.5, 1.0, 1.5, 2.0, 3.0, 4.0, 6.0, -0.0, -0.5, -1.0, -1.5, -2.0, -3.0, -4.0, -6.0])


def pack_weight(w, fmt):
    k, n = w.shape
    w = f64(np.asarray(w, np.float32).astype(ml_dtypes.bfloat16)).reshape(k // 32, 32, n)
    amax = np.abs(w).max(1)
    if fmt == "e4m3":
        byte = np.frexp(amax)[1] - 1 + 127 - 7
    else:
        mant, ex = np.frexp(amax / 6.0)
        byte = np.where(mant > 0.5, ex, ex - 1) + 127
    byte = np.clip(np.where(amax > 0, byte, 1), 1, 254)
    scaled = (w * np.exp2(127.0 - byte)[:, None, :]).reshape(k, n).astype(np.float32)
    by_word = np.ascontiguousarray(scaled.reshape(k // 512, 128, 4, n).transpose(0, 1, 3, 2))
    if fmt == "e4m3":
        words = by_word.astype(ml_dtypes.float8_e4m3fn).view(np.uint8)
    else:
        c = by_word.astype(ml_dtypes.float4_e2m1fn).view(np.uint8) & 0xF
        words = (c[..., 0::2] | (c[..., 1::2] << 4)).reshape(k // 512, 128, 2 * n)
    return np.ascontiguousarray(words), np.ascontiguousarray(byte.astype(np.uint8).reshape(k // 512, 16, n))


def unpack_weight(words, scales, fmt):
    g, _, n = scales.shape
    words = np.ascontiguousarray(words).reshape(g, 128, n, -1)
    if fmt == "e4m3":
        vals = words.view(ml_dtypes.float8_e4m3fn).astype(np.float64)
    else:
        nib = np.empty((g, 128, n, 4), np.uint8)
        nib[..., 0::2] = words & 0xF
        nib[..., 1::2] = words >> 4
        vals = E2M1[nib]
    vals = vals * np.repeat(np.exp2(scales.astype(np.float64) - 127.0), 8, axis=1)[..., None]
    return vals.transpose(0, 1, 3, 2).reshape(g * 512, n)


D, E, T, I, Q, G = 512, 512, 2048, 512, 128, 32


def setup_inputs():
    n = np.random.standard_normal
    idx = np.random.permutation(T)[:I]
    fd = mx_kscale(D)
    fe = mx_kscale(E)
    keysp = pack_weight(n((D, T)) / fd[:, None], "e4m3")
    valsp = pack_weight(n((E, T)) / fe[:, None], "e4m3")
    return {
        "query": (n((D, Q)) * 0.6 / np.sqrt(D) * fd[:, None]).astype(np.float32),
        "keys_words": keysp[0],
        "keys_scales": keysp[1],
        "trust": (np.random.uniform(0.3, 1.0, (Q, 1))).astype(np.float32),
        "gout": (n((E, Q)) * 1 / np.sqrt(E) * fe[:, None]).astype(np.float32),
        "vals_words": valsp[0],
        "vals_scales": valsp[1],
        "size": (np.random.uniform(0.5, 2.0, (1, I))).astype(np.float32),
        "base": (0.5 * n((Q, T))).astype(np.float32),
        "gq1": (np.random.uniform(0.3, 1.5, (Q, 1))).astype(np.float32),
        "offs": striped(idx),
    }


def reference(query, keys_words, keys_scales, trust, gout, vals_words, vals_scales, size, base, gq1, offs):
    idx = unstriped(offs)
    keysu = unpack_weight(keys_words, keys_scales, "e4m3")
    valsu = unpack_weight(vals_words, vals_scales, "e4m3")
    queryq = mxq(f64(query), 0, "e4m3")
    keysidxg = keysu[:, idx]
    a = queryq.T @ keysidxg
    s = a.reshape(Q, G, I // G).mean(axis=2) * f64(trust)
    sr = np.repeat(s, I // G, axis=1)
    b = a - sr
    p = np.exp(b - np.max(b, axis=1, keepdims=True))
    z = np.sum(p, axis=1, keepdims=True)
    goutq = mxq(f64(gout), 0, "e4m3")
    valsidxg = valsu[:, idx]
    c0 = goutq.T @ valsidxg
    dz = np.sum(c0 * p * f64(size) / np.square(z) * (-1.0), axis=1, keepdims=True)
    dp = c0 / z * f64(size) + dz
    db = dp * p
    dsr = db * (-1.0)
    ds = dsr.reshape(Q, G, I // G).sum(axis=2)
    e1 = ds * f64(trust) / 16.0
    r1 = np.repeat(e1, I // G, axis=1)
    da = db + r1
    hda = da * 512.0 * 2.0 * 512.0
    he1 = hda.reshape(Q, G, I // G).sum(axis=2)
    hds = he1 / 16.0 * f64(trust)
    r51 = np.repeat(hds, I // G, axis=1)
    hdb = hda - r51
    hdp = hdb * p
    hdz = np.sum(hdp, axis=1, keepdims=True)
    hz = np.sum(hdp * f64(size) * c0 / np.square(z) * (-1.0), axis=1, keepdims=True) + np.sum(hdz * (-1.0) * c0 * p * f64(size) / np.square(np.square(z)) * (-1.0), axis=1, keepdims=True) * z * 2.0
    hp = hdb * dp + hdz * (-1.0) / np.square(z) * c0 * f64(size) + hz
    hb = hp * p
    hsr = hb * (-1.0)
    hs = hsr.reshape(Q, G, I // G).sum(axis=2)
    e52 = hs * f64(trust) / 16.0
    r52 = np.repeat(e52, I // G, axis=1)
    ha = hb + r52
    gs = ha * f64(gq1)
    gf = np.zeros((Q, T))
    gf[:, idx] = gs
    y = f64(base) + gf
    return y

@@ -1,0 +1,197 @@
+from contextlib import ExitStack
+
+import concourse.mybir as mybir
+
+D, E, T, I, Q, G = 512, 512, 2048, 512, 128, 32
+PAGE = I // G
+P = 128
+PACK = 4
+HALF = I // 2
+FLOPS = 2 * Q * I * (D + E)
+
+F32 = mybir.dt.float32
+BF16 = mybir.dt.bfloat16
+I32 = mybir.dt.int32
+U32 = mybir.dt.uint32
+U16 = mybir.dt.uint16
+U8 = mybir.dt.uint8
+FP8X4 = mybir.dt.float8_e4m3fn_x4
+ALU = mybir.AluOpType
+ACT = mybir.ActivationFunctionType
+AX = mybir.AxisListType
+
+PENALTY = 512.0 * 2.0 * 512.0
+OUT_CHUNKS = (256, 512, 512, 512, 256)
+
+
+def by_page(ap):
+    return ap.rearrange("p (g j) -> p g j", j=PAGE)
+
+
+def over_page(ap, pages):
+    return ap.unsqueeze(2).to_broadcast([P, pages, PAGE])
+
+
+def tile_attend_gppagecentred_kernel(
+    tc, query, keys_words, keys_scales, trust, gout, vals_words, vals_scales, size, base, gq1, offs, out
+):
+    nc = tc.nc
+    halves = [slice(0, HALF), slice(HALF, I)]
+    page_halves = [slice(0, G // 2), slice(G // 2, G)]
+    off_halves = [slice(0, HALF // 16), slice(HALF // 16, I // 16)]
+
+    with ExitStack() as ctx:
+        sb = ctx.enter_context(tc.tile_pool(name="sb", bufs=1))
+        ps = ctx.enter_context(tc.psum_pool(name="ps", bufs=1))
+
+        offsets = sb.tile([P, I // 16], U16, name="offsets")
+        k_scales = sb.tile([P, T], U8, name="k_scales", align_bytes=64)
+        v_scales = sb.tile([P, T], U8, name="v_scales", align_bytes=64)
+        k_words = sb.tile([P, T], I32, name="k_words", align_bytes=64)
+        v_words = sb.tile([P, T], I32, name="v_words", tag="v_words", align_bytes=64)
+        q_raw = sb.tile([P, PACK, Q], F32, name="q_raw")
+        g_raw = sb.tile([P, PACK, Q], F32, name="g_raw")
+        size_t = sb.tile([P, I], F32, name="size_t")
+        base_t = sb.tile([P, T], F32, name="base_t")
+        trust_t = sb.tile([P, 1], F32, name="trust_t")
+        gq1_t = sb.tile([P, 1], F32, name="gq1_t")
+        placed = sb.tile([P, T], F32, name="placed")
+        warm = sb.tile([P, 1], F32, name="warm")
+        warm_out = sb.tile([P, 1], F32, name="warm_out")
+
+        nc.vector.memset(k_scales[:].bitcast(I32), 0)
+        nc.vector.memset(warm[:], 0.0)
+        nc.vector.memset(v_scales[:].bitcast(I32), 0)
+        nc.vector.memset(placed[:], 0.0)
+        nc.scalar.activation(warm_out[:], warm[:], ACT.Exp)
+
+        def load_scales(dst, src):
+            for r in range(4):
+                nc.sync.dma_start(dst[r:P:32, :].bitcast(I32), src[0, r:16:4, :].bitcast(I32))
+
+        def load_words(dst, src):
+            nc.sync.dma_start(dst[:], src[0].rearrange("p n t -> p (n t)").bitcast(I32))
+
+        nc.sync.dma_start(offsets[:], offs)
+        load_scales(k_scales, keys_scales)
+        nc.sync.dma_start(q_raw[:], query.rearrange("(p j) w -> p j w", j=PACK))
+        load_words(k_words, keys_words)
+        load_scales(v_scales, vals_scales)
+        nc.gpsimd.dma_start(trust_t[:], trust)
+        nc.gpsimd.dma_start(gq1_t[:], gq1)
+        nc.sync.dma_start(g_raw[:], gout.rearrange("(p j) w -> p j w", j=PACK))
+        load_words(v_words, vals_words)
+        nc.sync.dma_start(size_t[:], size[0].partition_broadcast(P))
+        nc.sync.dma_start(base_t[:], base)
+
+        def interleave(raw, name):
+            grouped = sb.tile([P, Q, PACK], BF16, name=name + "_bf", align_bytes=64)
+            nc.scalar.copy(grouped[:], raw[:].rearrange("p j w -> p w j"))
+            return grouped
+
+        def quantize(grouped, name):
+            codes = sb.tile([P, Q], U32, name=name + "_codes", align_bytes=64)
+            scales = sb.tile([P, Q], U8, name=name + "_mxs", align_bytes=64)
+            nc.vector.quantize_mx(
+                out=codes[:].bitcast(FP8X4), scales=scales[:], in_=grouped[:].rearrange("p w j -> p (w j)")
+            )
+            return codes, scales
+
+        def small(name, width=1):
+            return sb.tile([P, width], F32, name=name)
+
+        def wide(name):
+            return sb.tile([P, I], F32, name=name)
+
+        q_bf = interleave(q_raw, "q")
+        nt16, t16, nt8, ntau16, factor = (small(n) for n in ("nt16", "t16", "nt8", "ntau16", "factor"))
+        nc.scalar.mul(nt16[:], trust_t[:], -1.0 / PAGE)
+        nc.scalar.mul(t16[:], trust_t[:], 1.0 / PAGE)
+        nc.scalar.mul(nt8[:], trust_t[:], -2.0 / PAGE)
+        nc.scalar.activation(ntau16[:], trust_t[:], ACT.Identity, bias=nt8[:], scale=t16[:])
+        nc.scalar.mul(factor[:], gq1_t[:], -PENALTY)
+        g_bf = interleave(g_raw, "g")
+
+        kg_scales = sb.tile([P, I], U8, name="kg_scales", align_bytes=64)
+        vg_scales = sb.tile([P, I], U8, name="vg_scales", align_bytes=64)
+        kg_words = sb.tile([P, I], U32, name="kg_words", align_bytes=64)
+        vg_words = sb.tile([P, I], U32, name="vg_words", align_bytes=64)
+
+        nc.vector.tensor_copy(kg_scales[:], k_scales[:].indirect(offsets[:]))
+        for h in range(2):
+            nc.vector.tensor_copy(kg_words[:, halves[h]], k_words[:].bitcast(U32).indirect(offsets[:, off_halves[h]]))
+        q_codes, q_mxs = quantize(q_bf, "q")
+        nc.vector.tensor_copy(vg_scales[:], v_scales[:].indirect(offsets[:]))
+
+        a_ps = [ps.tile([P, HALF], F32, name="a_ps%d" % h) for h in range(2)]
+        for h in range(2):
+            nc.tensor.matmul_mx(
+                out=a_ps[h][:], lhsT=q_codes[:].bitcast(FP8X4), lhsT_scale=q_mxs[:],
+                rhs=kg_words[:, halves[h]].bitcast(FP8X4), rhs_scale=kg_scales[:, halves[h]],
+                start=True, stop=True,
+            )
+
+        a_sum = small("a_sum", G)
+        b = wide("b")
+        for h in range(2):
+            nc.vector.tensor_reduce(a_sum[:, page_halves[h]], by_page(a_ps[h][:]), AX.X, ALU.add)
+        for h in range(2):
+            nc.vector.scalar_tensor_tensor(
+                by_page(b[:, halves[h]]), over_page(a_sum[:, page_halves[h]], G // 2), nt16[:], by_page(a_ps[h][:]),
+                ALU.mult, ALU.add,
+            )
+        g_codes, g_mxs = quantize(g_bf, "g")
+        neg_max, z = small("neg_max"), small("z")
+        nc.vector.tensor_reduce(neg_max[:], b[:], AX.X, ALU.max, negate=True)
+        p = wide("p")
+        nc.scalar.activation(p[:], b[:], ACT.Exp, bias=neg_max[:], accum_out=z[:])
+
+        c_ps = ps.tile([P, I], F32, name="c_ps")
+        for h in range(2):
+            nc.vector.tensor_copy(vg_words[:, halves[h]], v_words[:].bitcast(U32).indirect(offsets[:, off_halves[h]]))
+            nc.tensor.matmul_mx(
+                out=c_ps[:, halves[h]], lhsT=g_codes[:].bitcast(FP8X4), lhsT_scale=g_mxs[:],
+                rhs=vg_words[:, halves[h]].bitcast(FP8X4), rhs_scale=vg_scales[:, halves[h]],
+                start=True, stop=True,
+            )
+
+        rz = sb.tile([P, 1], F32, name="rz", tag="v_words", align_bytes=64)
+        nc.vector.reciprocal(rz[:], z[:])
+        pi, pi_size, e, w, w_f, hh, junk, y, hb, spread = (
+            wide(n) for n in ("pi", "pi_size", "e", "w", "w_f", "hh", "junk", "y", "hb", "spread")
+        )
+        nc.scalar.mul(pi[:], p[:], rz[:])
+        nc.vector.scalar_tensor_tensor(pi_size[:], p[:], rz[:], size_t[:], ALU.mult, ALU.mult)
+        m, h1, h3 = small("m"), small("h1"), small("h3")
+        nc.vector.scalar_tensor_tensor(e[:], c_ps[:], 1.0, pi_size[:], ALU.mult, ALU.mult, accum_out=m[:])
+        w_sum, hb_sum = small("w_sum", G), small("hb_sum", G)
+        for h in range(2):
+            s = halves[h]
+            nc.vector.scalar_tensor_tensor(w[:, s], pi[:, s], m[:], e[:, s], ALU.mult, ALU.subtract)
+        nc.scalar.mul(w_f[:], w[:], factor[:])
+        for h in range(2):
+            nc.vector.tensor_reduce(w_sum[:, page_halves[h]], by_page(w[:, halves[h]]), AX.X, ALU.add)
+        for h in range(2):
+            nc.vector.scalar_tensor_tensor(
+                by_page(hh[:, halves[h]]), over_page(w_sum[:, page_halves[h]], G // 2), ntau16[:],
+                by_page(w[:, halves[h]]), ALU.mult, ALU.add,
+            )
+        nc.vector.scalar_tensor_tensor(junk[:], hh[:], 1.0, pi[:], ALU.mult, ALU.mult, accum_out=h1[:])
+        nc.vector.scalar_tensor_tensor(y[:], hh[:], h1[:], w_f[:], ALU.subtract, ALU.mult, accum_out=h3[:])
+        for h in range(2):
+            s = halves[h]
+            nc.vector.scalar_tensor_tensor(hb[:, s], pi[:, s], h3[:], y[:, s], ALU.mult, ALU.subtract)
+        for h in range(2):
+            nc.vector.tensor_reduce(hb_sum[:, page_halves[h]], by_page(hb[:, halves[h]]), AX.X, ALU.add)
+            nc.scalar.mul(by_page(spread[:, halves[h]]), over_page(hb_sum[:, page_halves[h]], G // 2), nt16[:])
+        for h in range(2):
+            s = halves[h]
+            nc.vector.tensor_tensor(placed[:].indirect(offsets[:, off_halves[h]]), hb[:, s], spread[:, s], ALU.add)
+
+        result = sb.tile([P, T], F32, name="result")
+        start = 0
+        for width in OUT_CHUNKS:
+            s = slice(start, start + width)
+            nc.vector.tensor_tensor(result[:, s], placed[:, s], base_t[:, s], ALU.add)
+            nc.sync.dma_start(out[:, s], result[:, s])
+            start += width

@@ -1,6 +1,7 @@
 from contextlib import ExitStack
 
 import concourse.mybir as mybir
+from concourse.masks import make_identity
 
 D, E, T, I, Q, G = 512, 512, 2048, 512, 128, 32
 PAGE = I // G
@@ -46,12 +47,13 @@ def tile_attend_gppagecentred_kernel(
 
         offsets = sb.tile([P, I // 16], U16, name="offsets")
         k_scales = sb.tile([P, T], U8, name="k_scales", align_bytes=64)
-        v_scales = sb.tile([P, T], U8, name="v_scales", align_bytes=64)
+        v_scales = sb.tile([P, T], U8, name="v_scales", tag="v_scales", align_bytes=64)
         k_words = sb.tile([P, T], I32, name="k_words", align_bytes=64)
         v_words = sb.tile([P, T], I32, name="v_words", tag="v_words", align_bytes=64)
         q_raw = sb.tile([P, PACK, Q], F32, name="q_raw")
-        g_raw = sb.tile([P, PACK, Q], F32, name="g_raw")
-        size_t = sb.tile([P, I], F32, name="size_t")
+        g_raw = sb.tile([P, PACK, Q], F32, name="g_raw", tag="g_raw")
+        size_t = sb.tile([P, PACK], F32, name="size_t")
+        identity = sb.tile([P, P], F32, name="identity")
         base_t = sb.tile([P, T], F32, name="base_t")
         trust_t = sb.tile([P, 1], F32, name="trust_t")
         gq1_t = sb.tile([P, 1], F32, name="gq1_t")
@@ -59,11 +61,12 @@ def tile_attend_gppagecentred_kernel(
         warm = sb.tile([P, 1], F32, name="warm")
         warm_out = sb.tile([P, 1], F32, name="warm_out")
 
-        nc.vector.memset(k_scales[:].bitcast(I32), 0)
-        nc.vector.memset(warm[:], 0.0)
+        nc.gpsimd.memset(k_scales[:].bitcast(I32), 0)
         nc.vector.memset(v_scales[:].bitcast(I32), 0)
+        nc.vector.memset(warm[:], 0.0)
         nc.vector.memset(placed[:], 0.0)
         nc.scalar.activation(warm_out[:], warm[:], ACT.Exp)
+        make_identity(nc, identity[:])
 
         def load_scales(dst, src):
             for r in range(4):
@@ -77,15 +80,15 @@ def tile_attend_gppagecentred_kernel(
         nc.sync.dma_start(q_raw[:], query.rearrange("(p j) w -> p j w", j=PACK))
         load_words(k_words, keys_words)
         load_scales(v_scales, vals_scales)
-        nc.gpsimd.dma_start(trust_t[:], trust)
-        nc.gpsimd.dma_start(gq1_t[:], gq1)
+        nc.sync.dma_start(trust_t[:], trust)
+        nc.sync.dma_start(size_t[:], size[0].rearrange("(n m) -> n m", m=PACK))
         nc.sync.dma_start(g_raw[:], gout.rearrange("(p j) w -> p j w", j=PACK))
         load_words(v_words, vals_words)
-        nc.sync.dma_start(size_t[:], size[0].partition_broadcast(P))
+        nc.sync.dma_start(gq1_t[:], gq1)
         nc.sync.dma_start(base_t[:], base)
 
         def interleave(raw, name):
-            grouped = sb.tile([P, Q, PACK], BF16, name=name + "_bf", align_bytes=64)
+            grouped = sb.tile([P, Q, PACK], BF16, name=name + "_bf", tag=name + "_bf", align_bytes=64)
             nc.scalar.copy(grouped[:], raw[:].rearrange("p j w -> p w j"))
             return grouped
 
@@ -109,7 +112,6 @@ def tile_attend_gppagecentred_kernel(
         nc.scalar.mul(t16[:], trust_t[:], 1.0 / PAGE)
         nc.scalar.mul(nt8[:], trust_t[:], -2.0 / PAGE)
         nc.scalar.activation(ntau16[:], trust_t[:], ACT.Identity, bias=nt8[:], scale=t16[:])
-        nc.scalar.mul(factor[:], gq1_t[:], -PENALTY)
         g_bf = interleave(g_raw, "g")
 
         kg_scales = sb.tile([P, I], U8, name="kg_scales", align_bytes=64)
@@ -118,32 +120,36 @@ def tile_attend_gppagecentred_kernel(
         vg_words = sb.tile([P, I], U32, name="vg_words", align_bytes=64)
 
         nc.vector.tensor_copy(kg_scales[:], k_scales[:].indirect(offsets[:]))
+        q_codes, q_mxs = quantize(q_bf, "q")
         for h in range(2):
             nc.vector.tensor_copy(kg_words[:, halves[h]], k_words[:].bitcast(U32).indirect(offsets[:, off_halves[h]]))
-        q_codes, q_mxs = quantize(q_bf, "q")
         nc.vector.tensor_copy(vg_scales[:], v_scales[:].indirect(offsets[:]))
 
-        a_ps = [ps.tile([P, HALF], F32, name="a_ps%d" % h) for h in range(2)]
+        a_ps = ps.tile([P, I], F32, name="a_ps")
         for h in range(2):
             nc.tensor.matmul_mx(
-                out=a_ps[h][:], lhsT=q_codes[:].bitcast(FP8X4), lhsT_scale=q_mxs[:],
+                out=a_ps[:, halves[h]], lhsT=q_codes[:].bitcast(FP8X4), lhsT_scale=q_mxs[:],
                 rhs=kg_words[:, halves[h]].bitcast(FP8X4), rhs_scale=kg_scales[:, halves[h]],
                 start=True, stop=True,
             )
+        size_ps = ps.tile([P, PACK, P], F32, name="size_ps")
+        for j in range(PACK):
+            nc.tensor.transpose(size_ps[:, j, :], size_t[:, j : j + 1].to_broadcast([P, P]), identity[:])
 
-        a_sum = small("a_sum", G)
+        a_sum = sb.tile([P, G], F32, name="a_sum", tag="v_scales", align_bytes=64)
         b = wide("b")
         for h in range(2):
-            nc.vector.tensor_reduce(a_sum[:, page_halves[h]], by_page(a_ps[h][:]), AX.X, ALU.add)
+            nc.vector.tensor_reduce(a_sum[:, page_halves[h]], by_page(a_ps[:, halves[h]]), AX.X, ALU.add)
         for h in range(2):
             nc.vector.scalar_tensor_tensor(
-                by_page(b[:, halves[h]]), over_page(a_sum[:, page_halves[h]], G // 2), nt16[:], by_page(a_ps[h][:]),
+                by_page(b[:, halves[h]]), over_page(a_sum[:, page_halves[h]], G // 2), nt16[:], by_page(a_ps[:, halves[h]]),
                 ALU.mult, ALU.add,
             )
         g_codes, g_mxs = quantize(g_bf, "g")
-        neg_max, z = small("neg_max"), small("z")
+        neg_max = sb.tile([P, 1], F32, name="neg_max", tag="g_bf", align_bytes=64)
+        z = small("z")
         nc.vector.tensor_reduce(neg_max[:], b[:], AX.X, ALU.max, negate=True)
-        p = wide("p")
+        p = sb.tile([P, I], F32, name="p", tag="g_raw")
         nc.scalar.activation(p[:], b[:], ACT.Exp, bias=neg_max[:], accum_out=z[:])
 
         c_ps = ps.tile([P, I], F32, name="c_ps")
@@ -155,38 +161,53 @@ def tile_attend_gppagecentred_kernel(
                 start=True, stop=True,
             )
 
-        rz = sb.tile([P, 1], F32, name="rz", tag="v_words", align_bytes=64)
-        nc.vector.reciprocal(rz[:], z[:])
-        pi, pi_size, e, w, w_f, hh, junk, y, hb, spread = (
-            wide(n) for n in ("pi", "pi_size", "e", "w", "w_f", "hh", "junk", "y", "hb", "spread")
+        p_size, rz = wide("p_size")[:], small("rz")[:]
+        nc.vector.reciprocal(rz, z[:])
+        pi, e, w, w_f, hh, junk, y, pi_c, pi_term, y_term = (
+            wide(n) for n in ("pi", "e", "w", "w_f", "hh", "junk", "y", "pi_c", "pi_term", "y_term")
         )
-        nc.scalar.mul(pi[:], p[:], rz[:])
-        nc.vector.scalar_tensor_tensor(pi_size[:], p[:], rz[:], size_t[:], ALU.mult, ALU.mult)
         m, h1, h3 = small("m"), small("h1"), small("h3")
-        nc.vector.scalar_tensor_tensor(e[:], c_ps[:], 1.0, pi_size[:], ALU.mult, ALU.mult, accum_out=m[:])
-        w_sum, hb_sum = small("w_sum", G), small("hb_sum", G)
+        w_sum, y_sum, pi_sum = small("w_sum", G), small("y_sum", G), small("pi_sum", G)
+
+        def page_sum(dst, src, h):
+            nc.vector.tensor_reduce(dst[:, page_halves[h]], by_page(src[:, halves[h]]), AX.X, ALU.add)
+
+        def centre(dst, sums, coeff, src, h, op):
+            nc.vector.scalar_tensor_tensor(
+                by_page(dst[:, halves[h]]), over_page(sums[:, page_halves[h]], G // 2), coeff[:],
+                by_page(src[:, halves[h]]), ALU.mult, op,
+            )
+
+        nc.scalar.mul(pi[:], p[:], rz)
+        nc.scalar.mul(factor[:], gq1_t[:], -PENALTY)
+        nc.vector.tensor_tensor(
+            p_size.rearrange("p (n m) -> p n m", m=PACK), p[:].rearrange("p (n m) -> p n m", m=PACK),
+            size_ps[:].rearrange("p m n -> p n m"), ALU.mult,
+        )
+        nc.vector.scalar_tensor_tensor(e[:], c_ps[:], rz, p_size, ALU.mult, ALU.mult, accum_out=m[:])
+        page_sum(pi_sum, pi, 0)
         for h in range(2):
             s = halves[h]
             nc.vector.scalar_tensor_tensor(w[:, s], pi[:, s], m[:], e[:, s], ALU.mult, ALU.subtract)
         nc.scalar.mul(w_f[:], w[:], factor[:])
         for h in range(2):
-            nc.vector.tensor_reduce(w_sum[:, page_halves[h]], by_page(w[:, halves[h]]), AX.X, ALU.add)
+            page_sum(w_sum, w, h)
         for h in range(2):
-            nc.vector.scalar_tensor_tensor(
-                by_page(hh[:, halves[h]]), over_page(w_sum[:, page_halves[h]], G // 2), ntau16[:],
-                by_page(w[:, halves[h]]), ALU.mult, ALU.add,
-            )
+            centre(hh, w_sum, ntau16, w, h, ALU.add)
+        page_sum(pi_sum, pi, 1)
         nc.vector.scalar_tensor_tensor(junk[:], hh[:], 1.0, pi[:], ALU.mult, ALU.mult, accum_out=h1[:])
+        centre(pi_c, pi_sum, nt16, pi, 0, ALU.add)
         nc.vector.scalar_tensor_tensor(y[:], hh[:], h1[:], w_f[:], ALU.subtract, ALU.mult, accum_out=h3[:])
+        centre(pi_c, pi_sum, nt16, pi, 1, ALU.add)
+        for h in range(2):
+            nc.scalar.mul(pi_term[:, halves[h]], pi_c[:, halves[h]], h3[:])
+        for h in range(2):
+            page_sum(y_sum, y, h)
+        for h in range(2):
+            centre(y_term, y_sum, t16, y, h, ALU.subtract)
         for h in range(2):
             s = halves[h]
-            nc.vector.scalar_tensor_tensor(hb[:, s], pi[:, s], h3[:], y[:, s], ALU.mult, ALU.subtract)
-        for h in range(2):
-            nc.vector.tensor_reduce(hb_sum[:, page_halves[h]], by_page(hb[:, halves[h]]), AX.X, ALU.add)
-            nc.scalar.mul(by_page(spread[:, halves[h]]), over_page(hb_sum[:, page_halves[h]], G // 2), nt16[:])
-        for h in range(2):
-            s = halves[h]
-            nc.vector.tensor_tensor(placed[:].indirect(offsets[:, off_halves[h]]), hb[:, s], spread[:, s], ALU.add)
+            nc.vector.tensor_tensor(placed[:].indirect(offsets[:, off_halves[h]]), y_term[:, s], pi_term[:, s], ALU.add)
 
         result = sb.tile([P, T], F32, name="result")
         start = 0

@@ -22,7 +22,7 @@ ACT = mybir.ActivationFunctionType
 AX = mybir.AxisListType
 
 PENALTY = 512.0 * 2.0 * 512.0
-OUT_CHUNKS = (256, 512, 512, 512, 256)
+OUT_CHUNKS = (384, 512, 448, 384, 192, 128)
 
 
 def by_page(ap):
@@ -205,9 +205,7 @@ def tile_attend_gppagecentred_kernel(
             page_sum(y_sum, y, h)
         for h in range(2):
             centre(y_term, y_sum, t16, y, h, ALU.subtract)
-        for h in range(2):
-            s = halves[h]
-            nc.vector.tensor_tensor(placed[:].indirect(offsets[:, off_halves[h]]), y_term[:, s], pi_term[:, s], ALU.add)
+        nc.vector.tensor_tensor(placed[:].indirect(offsets[:]), y_term[:], pi_term[:], ALU.add)
 
         result = sb.tile([P, T], F32, name="result")
         start = 0

@@ -47,7 +47,7 @@ def tile_attend_gppagecentred_kernel(
 
         offsets = sb.tile([P, I // 16], U16, name="offsets")
         k_scales = sb.tile([P, T], U8, name="k_scales", align_bytes=64)
-        v_scales = sb.tile([P, T], U8, name="v_scales", tag="v_scales", align_bytes=64)
+        v_scales = sb.tile([P, T], U8, name="v_scales", align_bytes=64)
         k_words = sb.tile([P, T], I32, name="k_words", align_bytes=64)
         v_words = sb.tile([P, T], I32, name="v_words", tag="v_words", align_bytes=64)
         q_raw = sb.tile([P, PACK, Q], F32, name="q_raw")
@@ -55,17 +55,13 @@ def tile_attend_gppagecentred_kernel(
         size_t = sb.tile([P, PACK], F32, name="size_t")
         identity = sb.tile([P, P], F32, name="identity")
         base_t = sb.tile([P, T], F32, name="base_t")
-        trust_t = sb.tile([P, 1], F32, name="trust_t")
+        trust_t = sb.tile([P, 1], F32, name="trust_t", tag="trust_t")
         gq1_t = sb.tile([P, 1], F32, name="gq1_t")
         placed = sb.tile([P, T], F32, name="placed")
-        warm = sb.tile([P, 1], F32, name="warm")
-        warm_out = sb.tile([P, 1], F32, name="warm_out")
 
         nc.gpsimd.memset(k_scales[:].bitcast(I32), 0)
         nc.vector.memset(v_scales[:].bitcast(I32), 0)
-        nc.vector.memset(warm[:], 0.0)
         nc.vector.memset(placed[:], 0.0)
-        nc.scalar.activation(warm_out[:], warm[:], ACT.Exp)
         make_identity(nc, identity[:])
 
         def load_scales(dst, src):
@@ -136,7 +132,7 @@ def tile_attend_gppagecentred_kernel(
         for j in range(PACK):
             nc.tensor.transpose(size_ps[:, j, :], size_t[:, j : j + 1].to_broadcast([P, P]), identity[:])
 
-        a_sum = sb.tile([P, G], F32, name="a_sum", tag="v_scales", align_bytes=64)
+        a_sum = sb.tile([P, G], F32, name="a_sum", tag="trust_t")
         b = wide("b")
         for h in range(2):
             nc.vector.tensor_reduce(a_sum[:, page_halves[h]], by_page(a_ps[:, halves[h]]), AX.X, ALU.add)
@@ -146,11 +142,10 @@ def tile_attend_gppagecentred_kernel(
                 ALU.mult, ALU.add,
             )
         g_codes, g_mxs = quantize(g_bf, "g")
-        neg_max = sb.tile([P, 1], F32, name="neg_max", tag="g_bf", align_bytes=64)
-        z = small("z")
-        nc.vector.tensor_reduce(neg_max[:], b[:], AX.X, ALU.max, negate=True)
-        p = sb.tile([P, I], F32, name="p", tag="g_raw")
-        nc.scalar.activation(p[:], b[:], ACT.Exp, bias=neg_max[:], accum_out=z[:])
+        p_and_max = sb.tile([P, I + 8], F32, name="p_and_max", tag="g_raw")
+        p, neg_max, z = p_and_max[:, 0:I], p_and_max[:, I : I + 1], small("z")
+        nc.vector.tensor_reduce(neg_max, b[:], AX.X, ALU.max, negate=True)
+        nc.scalar.activation(p, b[:], ACT.Exp, bias=neg_max, accum_out=z[:])
 
         c_ps = ps.tile([P, I], F32, name="c_ps")
         for h in range(2):
@@ -178,14 +173,17 @@ def tile_attend_gppagecentred_kernel(
                 by_page(src[:, halves[h]]), ALU.mult, op,
             )
 
-        nc.scalar.mul(pi[:], p[:], rz)
+        nt16_rz, h3_halves = small("nt16_rz"), small("h3_halves", 2)
+        nc.scalar.mul(pi[:], p, rz)
+        nc.scalar.mul(nt16_rz[:], nt16[:], rz)
         nc.scalar.mul(factor[:], gq1_t[:], -PENALTY)
         nc.vector.tensor_tensor(
-            p_size.rearrange("p (n m) -> p n m", m=PACK), p[:].rearrange("p (n m) -> p n m", m=PACK),
+            p_size.rearrange("p (n m) -> p n m", m=PACK), p.rearrange("p (n m) -> p n m", m=PACK),
             size_ps[:].rearrange("p m n -> p n m"), ALU.mult,
         )
+        page_sum(pi_sum, p, 0)
         nc.vector.scalar_tensor_tensor(e[:], c_ps[:], rz, p_size, ALU.mult, ALU.mult, accum_out=m[:])
-        page_sum(pi_sum, pi, 0)
+        page_sum(pi_sum, p, 1)
         for h in range(2):
             s = halves[h]
             nc.vector.scalar_tensor_tensor(w[:, s], pi[:, s], m[:], e[:, s], ALU.mult, ALU.subtract)
@@ -194,13 +192,16 @@ def tile_attend_gppagecentred_kernel(
             page_sum(w_sum, w, h)
         for h in range(2):
             centre(hh, w_sum, ntau16, w, h, ALU.add)
-        page_sum(pi_sum, pi, 1)
+        centre(pi_c, pi_sum, nt16_rz, pi, 0, ALU.add)
         nc.vector.scalar_tensor_tensor(junk[:], hh[:], 1.0, pi[:], ALU.mult, ALU.mult, accum_out=h1[:])
-        centre(pi_c, pi_sum, nt16, pi, 0, ALU.add)
-        nc.vector.scalar_tensor_tensor(y[:], hh[:], h1[:], w_f[:], ALU.subtract, ALU.mult, accum_out=h3[:])
-        centre(pi_c, pi_sum, nt16, pi, 1, ALU.add)
+        centre(pi_c, pi_sum, nt16_rz, pi, 1, ALU.add)
         for h in range(2):
-            nc.scalar.mul(pi_term[:, halves[h]], pi_c[:, halves[h]], h3[:])
+            s = halves[h]
+            nc.vector.scalar_tensor_tensor(
+                y[:, s], hh[:, s], h1[:], w_f[:, s], ALU.subtract, ALU.mult, accum_out=h3_halves[:, h : h + 1]
+            )
+        nc.scalar.activation(h3[:], h3_halves[:, 0:1], ACT.Identity, bias=h3_halves[:, 1:2])
+        nc.scalar.mul(pi_term[:], pi_c[:], h3[:])
         for h in range(2):
             page_sum(y_sum, y, h)
         for h in range(2):

from contextlib import ExitStack

import concourse.mybir as mybir
from concourse.masks import make_identity

D, E, T, I, Q, G = 512, 512, 2048, 512, 128, 32
PAGE = I // G
P = 128
PACK = 4
HALF = I // 2
FLOPS = 2 * Q * I * (D + E)

F32 = mybir.dt.float32
BF16 = mybir.dt.bfloat16
I32 = mybir.dt.int32
U32 = mybir.dt.uint32
U16 = mybir.dt.uint16
U8 = mybir.dt.uint8
FP8X4 = mybir.dt.float8_e4m3fn_x4
ALU = mybir.AluOpType
ACT = mybir.ActivationFunctionType
AX = mybir.AxisListType

PENALTY = 512.0 * 2.0 * 512.0
OUT_CHUNKS = (384, 512, 448, 384, 192, 128)


def by_page(ap):
    return ap.rearrange("p (g j) -> p g j", j=PAGE)


def over_page(ap, pages):
    return ap.unsqueeze(2).to_broadcast([P, pages, PAGE])


def tile_attend_gppagecentred_kernel(
    tc, query, keys_words, keys_scales, trust, gout, vals_words, vals_scales, size, base, gq1, offs, out
):
    nc = tc.nc
    halves = [slice(0, HALF), slice(HALF, I)]
    page_halves = [slice(0, G // 2), slice(G // 2, G)]
    off_halves = [slice(0, HALF // 16), slice(HALF // 16, I // 16)]

    with ExitStack() as ctx:
        sb = ctx.enter_context(tc.tile_pool(name="sb", bufs=1))
        ps = ctx.enter_context(tc.psum_pool(name="ps", bufs=1))

        offsets = sb.tile([P, I // 16], U16, name="offsets")
        k_scales = sb.tile([P, T], U8, name="k_scales", align_bytes=64)
        v_scales = sb.tile([P, T], U8, name="v_scales", align_bytes=64)
        k_words = sb.tile([P, T], I32, name="k_words", align_bytes=64)
        v_words = sb.tile([P, T], I32, name="v_words", tag="v_words", align_bytes=64)
        q_raw = sb.tile([P, PACK, Q], F32, name="q_raw")
        g_raw = sb.tile([P, PACK, Q], F32, name="g_raw", tag="g_raw")
        size_t = sb.tile([P, PACK], F32, name="size_t")
        identity = sb.tile([P, P], F32, name="identity")
        base_t = sb.tile([P, T], F32, name="base_t")
        trust_t = sb.tile([P, 1], F32, name="trust_t", tag="trust_t")
        gq1_t = sb.tile([P, 1], F32, name="gq1_t")
        placed = sb.tile([P, T], F32, name="placed")

        nc.gpsimd.memset(k_scales[:].bitcast(I32), 0)
        nc.vector.memset(v_scales[:].bitcast(I32), 0)
        nc.vector.memset(placed[:], 0.0)
        make_identity(nc, identity[:])

        def load_scales(dst, src):
            for r in range(4):
                nc.sync.dma_start(dst[r:P:32, :].bitcast(I32), src[0, r:16:4, :].bitcast(I32))

        def load_words(dst, src):
            nc.sync.dma_start(dst[:], src[0].rearrange("p n t -> p (n t)").bitcast(I32))

        nc.sync.dma_start(offsets[:], offs)
        load_scales(k_scales, keys_scales)
        nc.sync.dma_start(q_raw[:], query.rearrange("(p j) w -> p j w", j=PACK))
        load_words(k_words, keys_words)
        load_scales(v_scales, vals_scales)
        nc.sync.dma_start(trust_t[:], trust)
        nc.sync.dma_start(size_t[:], size[0].rearrange("(n m) -> n m", m=PACK))
        nc.sync.dma_start(g_raw[:], gout.rearrange("(p j) w -> p j w", j=PACK))
        load_words(v_words, vals_words)
        nc.sync.dma_start(gq1_t[:], gq1)
        nc.sync.dma_start(base_t[:], base)

        def interleave(raw, name):
            grouped = sb.tile([P, Q, PACK], BF16, name=name + "_bf", tag=name + "_bf", align_bytes=64)
            nc.scalar.copy(grouped[:], raw[:].rearrange("p j w -> p w j"))
            return grouped

        def quantize(grouped, name):
            codes = sb.tile([P, Q], U32, name=name + "_codes", align_bytes=64)
            scales = sb.tile([P, Q], U8, name=name + "_mxs", align_bytes=64)
            nc.vector.quantize_mx(
                out=codes[:].bitcast(FP8X4), scales=scales[:], in_=grouped[:].rearrange("p w j -> p (w j)")
            )
            return codes, scales

        def small(name, width=1):
            return sb.tile([P, width], F32, name=name)

        def wide(name):
            return sb.tile([P, I], F32, name=name)

        q_bf = interleave(q_raw, "q")
        nt16, t16, nt8, ntau16, factor = (small(n) for n in ("nt16", "t16", "nt8", "ntau16", "factor"))
        nc.scalar.mul(nt16[:], trust_t[:], -1.0 / PAGE)
        nc.scalar.mul(t16[:], trust_t[:], 1.0 / PAGE)
        nc.scalar.mul(nt8[:], trust_t[:], -2.0 / PAGE)
        nc.scalar.activation(ntau16[:], trust_t[:], ACT.Identity, bias=nt8[:], scale=t16[:])
        g_bf = interleave(g_raw, "g")

        kg_scales = sb.tile([P, I], U8, name="kg_scales", align_bytes=64)
        vg_scales = sb.tile([P, I], U8, name="vg_scales", align_bytes=64)
        kg_words = sb.tile([P, I], U32, name="kg_words", align_bytes=64)
        vg_words = sb.tile([P, I], U32, name="vg_words", align_bytes=64)

        nc.vector.tensor_copy(kg_scales[:], k_scales[:].indirect(offsets[:]))
        q_codes, q_mxs = quantize(q_bf, "q")
        for h in range(2):
            nc.vector.tensor_copy(kg_words[:, halves[h]], k_words[:].bitcast(U32).indirect(offsets[:, off_halves[h]]))
        nc.vector.tensor_copy(vg_scales[:], v_scales[:].indirect(offsets[:]))

        a_ps = ps.tile([P, I], F32, name="a_ps")
        for h in range(2):
            nc.tensor.matmul_mx(
                out=a_ps[:, halves[h]], lhsT=q_codes[:].bitcast(FP8X4), lhsT_scale=q_mxs[:],
                rhs=kg_words[:, halves[h]].bitcast(FP8X4), rhs_scale=kg_scales[:, halves[h]],
                start=True, stop=True,
            )
        size_ps = ps.tile([P, PACK, P], F32, name="size_ps")
        for j in range(PACK):
            nc.tensor.transpose(size_ps[:, j, :], size_t[:, j : j + 1].to_broadcast([P, P]), identity[:])

        a_sum = sb.tile([P, G], F32, name="a_sum", tag="trust_t")
        b = wide("b")
        for h in range(2):
            nc.vector.tensor_reduce(a_sum[:, page_halves[h]], by_page(a_ps[:, halves[h]]), AX.X, ALU.add)
        for h in range(2):
            nc.vector.scalar_tensor_tensor(
                by_page(b[:, halves[h]]), over_page(a_sum[:, page_halves[h]], G // 2), nt16[:], by_page(a_ps[:, halves[h]]),
                ALU.mult, ALU.add,
            )
        g_codes, g_mxs = quantize(g_bf, "g")
        p_and_max = sb.tile([P, I + 8], F32, name="p_and_max", tag="g_raw")
        p, neg_max, z = p_and_max[:, 0:I], p_and_max[:, I : I + 1], small("z")
        nc.vector.tensor_reduce(neg_max, b[:], AX.X, ALU.max, negate=True)
        nc.scalar.activation(p, b[:], ACT.Exp, bias=neg_max, accum_out=z[:])

        c_ps = ps.tile([P, I], F32, name="c_ps")
        for h in range(2):
            nc.vector.tensor_copy(vg_words[:, halves[h]], v_words[:].bitcast(U32).indirect(offsets[:, off_halves[h]]))
            nc.tensor.matmul_mx(
                out=c_ps[:, halves[h]], lhsT=g_codes[:].bitcast(FP8X4), lhsT_scale=g_mxs[:],
                rhs=vg_words[:, halves[h]].bitcast(FP8X4), rhs_scale=vg_scales[:, halves[h]],
                start=True, stop=True,
            )

        p_size, rz = wide("p_size")[:], small("rz")[:]
        nc.vector.reciprocal(rz, z[:])
        pi, e, w, w_f, hh, junk, y, pi_c, pi_term, y_term = (
            wide(n) for n in ("pi", "e", "w", "w_f", "hh", "junk", "y", "pi_c", "pi_term", "y_term")
        )
        m, h1, h3 = small("m"), small("h1"), small("h3")
        w_sum, y_sum, pi_sum = small("w_sum", G), small("y_sum", G), small("pi_sum", G)

        def page_sum(dst, src, h):
            nc.vector.tensor_reduce(dst[:, page_halves[h]], by_page(src[:, halves[h]]), AX.X, ALU.add)

        def centre(dst, sums, coeff, src, h, op):
            nc.vector.scalar_tensor_tensor(
                by_page(dst[:, halves[h]]), over_page(sums[:, page_halves[h]], G // 2), coeff[:],
                by_page(src[:, halves[h]]), ALU.mult, op,
            )

        nt16_rz, h3_halves = small("nt16_rz"), small("h3_halves", 2)
        nc.scalar.mul(pi[:], p, rz)
        nc.scalar.mul(nt16_rz[:], nt16[:], rz)
        nc.scalar.mul(factor[:], gq1_t[:], -PENALTY)
        nc.vector.tensor_tensor(
            p_size.rearrange("p (n m) -> p n m", m=PACK), p.rearrange("p (n m) -> p n m", m=PACK),
            size_ps[:].rearrange("p m n -> p n m"), ALU.mult,
        )
        page_sum(pi_sum, p, 0)
        nc.vector.scalar_tensor_tensor(e[:], c_ps[:], rz, p_size, ALU.mult, ALU.mult, accum_out=m[:])
        page_sum(pi_sum, p, 1)
        for h in range(2):
            s = halves[h]
            nc.vector.scalar_tensor_tensor(w[:, s], pi[:, s], m[:], e[:, s], ALU.mult, ALU.subtract)
        nc.scalar.mul(w_f[:], w[:], factor[:])
        for h in range(2):
            page_sum(w_sum, w, h)
        for h in range(2):
            centre(hh, w_sum, ntau16, w, h, ALU.add)
        centre(pi_c, pi_sum, nt16_rz, pi, 0, ALU.add)
        nc.vector.scalar_tensor_tensor(junk[:], hh[:], 1.0, pi[:], ALU.mult, ALU.mult, accum_out=h1[:])
        centre(pi_c, pi_sum, nt16_rz, pi, 1, ALU.add)
        for h in range(2):
            s = halves[h]
            nc.vector.scalar_tensor_tensor(
                y[:, s], hh[:, s], h1[:], w_f[:, s], ALU.subtract, ALU.mult, accum_out=h3_halves[:, h : h + 1]
            )
        nc.scalar.activation(h3[:], h3_halves[:, 0:1], ACT.Identity, bias=h3_halves[:, 1:2])
        nc.scalar.mul(pi_term[:], pi_c[:], h3[:])
        for h in range(2):
            page_sum(y_sum, y, h)
        for h in range(2):
            centre(y_term, y_sum, t16, y, h, ALU.subtract)
        nc.vector.tensor_tensor(placed[:].indirect(offsets[:]), y_term[:], pi_term[:], ALU.add)

        result = sb.tile([P, T], F32, name="result")
        start = 0
        for width in OUT_CHUNKS:
            s = slice(start, start + width)
            nc.vector.tensor_tensor(result[:, s], placed[:, s], base_t[:, s], ALU.add)
            nc.sync.dma_start(out[:, s], result[:, s])
            start += width
